import numpy as np
import ml_dtypes


def mxq(x, axis, fmt="e4m3"):
    dtype, down = {"e4m3": (ml_dtypes.float8_e4m3fn, 7), "e5m2": (ml_dtypes.float8_e5m2, 14)}[fmt]
    v = np.moveaxis(np.asarray(x, np.float32).astype(ml_dtypes.bfloat16).astype(np.float64), axis, -1)
    blocks = v.reshape(v.shape[:-1] + (-1, 32))
    amax = np.abs(blocks).max(-1, keepdims=True)
    byte = np.maximum(np.where(amax > 0, np.frexp(amax)[1] - 1 + 127, 0) - down, 1)
    scale = np.exp2(byte - 127.0)
    codes = (blocks / scale).astype(np.float32).astype(dtype).astype(np.float64)
    return np.moveaxis((codes * scale).reshape(v.shape), -1, axis)


WIDE = False


def mx_kscale(k):
    if not WIDE:
        return np.ones(k)
    levels = np.array([10, -10, 5, -5, 0])
    if k % 512:
        return np.exp2(np.random.permutation(np.resize(levels, k // 32))).repeat(32)
    a = np.empty((k // 512, 16))
    for p in range(k // 512):
        a[p, :8] = np.random.permutation(np.resize(levels, 8))
        for g in range(8):
            far = levels[np.abs(levels - a[p, g]) >= 10]
            a[p, g + 8] = far[np.random.randint(len(far))]
    return np.exp2(a.ravel()).repeat(32)


def f64(x):
    return np.asarray(x).astype(np.float64)


def striped(idx):
    return np.tile(idx.reshape(-1, 16).T, (8, 1)).astype(np.uint16)


def unstriped(offs):
    return offs[:16].T.reshape(-1).astype(np.int64)


E2M1 = np.array([0.0, 0.5, 1.0, 1.5, 2.0, 3.0, 4.0, 6.0, -0.0, -0.5, -1.0, -1.5, -2.0, -3.0, -4.0, -6.0])


def pack_weight(w, fmt):
    k, n = w.shape
    w = f64(np.asarray(w, np.float32).astype(ml_dtypes.bfloat16)).reshape(k // 32, 32, n)
    amax = np.abs(w).max(1)
    if fmt == "e4m3":
        byte = np.frexp(amax)[1] - 1 + 127 - 7
    else:
        mant, ex = np.frexp(amax / 6.0)
        byte = np.where(mant > 0.5, ex, ex - 1) + 127
    byte = np.clip(np.where(amax > 0, byte, 1), 1, 254)
    scaled = (w * np.exp2(127.0 - byte)[:, None, :]).reshape(k, n).astype(np.float32)
    by_word = np.ascontiguousarray(scaled.reshape(k // 512, 128, 4, n).transpose(0, 1, 3, 2))
    if fmt == "e4m3":
        words = by_word.astype(ml_dtypes.float8_e4m3fn).view(np.uint8)
    else:
        c = by_word.astype(ml_dtypes.float4_e2m1fn).view(np.uint8) & 0xF
        words = (c[..., 0::2] | (c[..., 1::2] << 4)).reshape(k // 512, 128, 2 * n)
    return np.ascontiguousarray(words), np.ascontiguousarray(byte.astype(np.uint8).reshape(k // 512, 16, n))


def unpack_weight(words, scales, fmt):
    g, _, n = scales.shape
    words = np.ascontiguousarray(words).reshape(g, 128, n, -1)
    if fmt == "e4m3":
        vals = words.view(ml_dtypes.float8_e4m3fn).astype(np.float64)
    else:
        nib = np.empty((g, 128, n, 4), np.uint8)
        nib[..., 0::2] = words & 0xF
        nib[..., 1::2] = words >> 4
        vals = E2M1[nib]
    vals = vals * np.repeat(np.exp2(scales.astype(np.float64) - 127.0), 8, axis=1)[..., None]
    return vals.transpose(0, 1, 3, 2).reshape(g * 512, n)


def gelu(v):
    return 0.5 * v * (1.0 + np.tanh(np.sqrt(2.0 / np.pi) * (v + 0.044715 * v**3)))


K, T, S, K2, H, N = 1024, 4096, 1024, 512, 1024, 256


def setup_inputs():
    n = np.random.standard_normal
    s = mx_kscale(K)[:, None]
    s2 = mx_kscale(K2)[:, None]
    u = mx_kscale(H)[:, None]
    d = {}
    d["tab_words"], d["tab_scales"] = pack_weight(n((K, T)) * s, "e4m3")
    d["offs"] = striped(np.random.permutation(T)[:S])
    d["xs_words"], d["xs_scales"] = pack_weight(n((K2, S)) * s2, "e4m3")
    d["w1"] = (n((K, H)) / s / K ** 0.5).astype(np.float32)
    d["w2_words"], d["w2_scales"] = pack_weight(n((K, H)) / s / K ** 0.5, "e2m1")
    d["w3"] = (0.9 * n((K2, H)) / s2 / K2 ** 0.5).astype(np.float32)
    d["gain"] = (np.exp(0.4 * n(H)) * u[:, 0]).astype(np.float32)
    d["w4"] = (n((H, N)) / u / H ** 0.5).astype(np.float32)
    d["b4"] = (0.6 * n(N)).astype(np.float32)
    return d


def reference(tab_words, tab_scales, offs, xs_words, xs_scales, w1, w2_words, w2_scales, w3, gain, w4, b4):
    v = unpack_weight(tab_words, tab_scales, "e4m3")[:, unstriped(offs)]
    xs = unpack_weight(xs_words, xs_scales, "e4m3")
    w2 = unpack_weight(w2_words, w2_scales, "e2m1")
    a = mxq(f64(w1), 0, "e4m3").T @ v
    b = w2.T @ v
    x = mxq(f64(w3), 0, "e4m3").T @ xs
    h = f64(gain)[:, None] * (np.tanh(a + x) - np.tanh(b - x))
    y = mxq(f64(w4), 0, "e4m3").T @ mxq(h, 0, "e4m3")
    return y + f64(b4)[:, None]

@@ -1,0 +1,307 @@
+from contextlib import ExitStack
+
+import concourse.mybir as mybir
+from concourse.masks import make_identity
+
+K, T, S, K2, H, N = 1024, 4096, 1024, 512, 1024, 256
+FLOPS = 2 * S * H * (K + K + K2 + N)
+
+F32 = mybir.dt.float32
+BF16 = mybir.dt.bfloat16
+I32 = mybir.dt.int32
+U32 = mybir.dt.uint32
+U16 = mybir.dt.uint16
+U8 = mybir.dt.uint8
+FP8X4 = mybir.dt.float8_e4m3fn_x4
+FP4X4 = mybir.dt.float4_e2m1fn_x4
+ACT = mybir.ActivationFunctionType
+ALU = mybir.AluOpType
+
+P = 128
+PASS = 512
+CHUNK = 256
+CHUNKS = S // CHUNK
+HALF = 512
+
+
+def tile_list_udder_health_scores_kernel(
+    tc, tab_words, tab_scales, offs, xs_words, xs_scales, w1, w2_words, w2_scales, w3, gain, w4, b4, out
+):
+    nc = tc.nc
+    with ExitStack() as ctx:
+        keep = ctx.enter_context(tc.tile_pool(name="keep", bufs=1))
+        work = ctx.enter_context(tc.tile_pool(name="work", bufs=3))
+        psum = ctx.enter_context(tc.psum_pool(name="psum", bufs=8))
+
+        def held(name, shape, dtype):
+            return keep.tile(shape, dtype, name=name, align_bytes=64)
+
+        offsets = keep.tile([P, S // 16], U16, name="offsets")
+        tab = [held("tab%d" % a, [P, T], U32) for a in range(2)]
+        tab_rows = held("tab_rows", [P, T], U8)
+        xs_codes = held("xs_codes", [P, S], U32)
+        xs_plane = held("xs_plane", [P, S], U8)
+        w2_raw = held("w2_raw", [P, 2, 2 * H], U8)
+        w2_raw_plane = held("w2_raw_plane", [P, 2, H], U8)
+        w2_codes = held("w2_codes", [P, 2, 2 * H], U8)
+        w2_plane = held("w2_plane", [P, 2, H], U8)
+        v_rows = held("v_rows", [P, S], U8)
+        v_plane = [held("v_plane%d" % a, [P, S], U8) for a in range(2)]
+        v0 = held("v0", [P, S], U32)
+        v1 = [held("v1_%d" % n, [P, HALF], U32) for n in range(2)]
+        vec_rows = held("vec_rows", [P, P], F32)
+        ident = held("ident", [P, P], F32)
+        consts = held("consts", [P, 16], F32)
+        w1_raw = [[held("w1_raw%d%d" % (b, a), [P, 4, PASS], F32) for a in range(2)] for b in range(2)]
+        w3_raw = [held("w3_raw%d" % b, [P, 4, PASS], F32) for b in range(2)]
+        w4_raw = held("w4_raw", [P, 2, 4, N], F32)
+
+        nc.vector.memset(xs_plane[:].bitcast(I32), 0)
+        nc.gpsimd.memset(tab_rows[32:64, :].bitcast(I32), 0)
+        nc.vector.memset(tab_rows[64:128, :].bitcast(I32), 0)
+        nc.vector.memset(w2_raw_plane[:].rearrange("p a c -> p (a c)").bitcast(I32), 0)
+        for a in range(2):
+            nc.vector.memset(v_plane[a][:].bitcast(I32), 0)
+        nc.vector.memset(vec_rows[:], 0.0)
+        make_identity(nc, ident[:])
+
+        def load_weight(dst, src, a, b):
+            rows = src[PASS * a : PASS * (a + 1), PASS * b : PASS * (b + 1)]
+            nc.sync.dma_start(out=dst[:], in_=rows.rearrange("(p j) c -> p j c", j=4))
+
+        def load_words(dst, src, lo, hi):
+            words = src.rearrange("p t i -> p (t i)").bitcast(I32)
+            nc.sync.dma_start(out=dst[:].bitcast(I32)[:, lo:hi], in_=words[:, lo:hi])
+
+        def move_rows(a, q):
+            row = 16 * a + 4 * q
+            nc.sync.dma_start(
+                out=v_plane[a][32 * q : 32 * q + 4, :].bitcast(I32), in_=v_rows[row : row + 4, :].bitcast(I32)
+            )
+
+        nc.sync.dma_start(
+            out=tab_rows[0:32, :].bitcast(I32), in_=tab_scales.rearrange("a q t -> (a q) t").bitcast(I32)
+        )
+        nc.sync.dma_start(offsets[:], offs)
+        load_weight(w3_raw[0], w3, 0, 0)
+        for q in range(4):
+            nc.sync.dma_start(
+                out=xs_plane[32 * q : 32 * q + 4, :].bitcast(I32), in_=xs_scales[0, 4 * q : 4 * q + 4, :].bitcast(I32)
+            )
+        load_words(xs_codes, xs_words[0], 0, S)
+        load_words(tab[0], tab_words[0], 0, T // 2)
+        for q in range(4):
+            nc.sync.dma_start(
+                out=w2_raw_plane[32 * q : 32 * q + 4, :, :].bitcast(I32),
+                in_=w2_scales[:, 4 * q : 4 * q + 4, :].rearrange("a r c -> r a c").bitcast(I32),
+            )
+        load_words(tab[0], tab_words[0], T // 2, T)
+        nc.vector.tensor_copy(out=v_rows[:], in_=tab_rows[:].indirect(offsets[:]))
+        for q in range(3):
+            move_rows(0, q)
+        nc.sync.dma_start(out=w2_raw[:].bitcast(I32), in_=w2_words.rearrange("a p c -> p a c").bitcast(I32))
+        move_rows(0, 3)
+        move_rows(1, 0)
+        load_words(tab[1], tab_words[1], 0, T // 2)
+        for q in range(1, 4):
+            move_rows(1, q)
+        load_words(tab[1], tab_words[1], T // 2, T)
+        for a in range(2):
+            load_weight(w1_raw[0][a], w1, a, 0)
+        for b in range(2):
+            nc.sync.dma_start(
+                out=vec_rows[4 * b : 4 * b + 4, :].rearrange("t (g i) -> t g i", i=4),
+                in_=gain[PASS * b : PASS * (b + 1)].rearrange("(g t i) -> t g i", t=4, i=4),
+            )
+        nc.sync.dma_start(out=vec_rows[8:10, :], in_=b4.rearrange("(m p) -> m p", p=P))
+        load_weight(w3_raw[1], w3, 0, 1)
+        for a in range(2):
+            load_weight(w1_raw[1][a], w1, a, 1)
+        for b in range(2):
+            for i in range(4):
+                nc.sync.dma_start(
+                    out=w4_raw[i:P:4, b, :, :],
+                    in_=w4[PASS * b : PASS * (b + 1), :].rearrange("(g t i) n -> i g t n", t=4, i=4)[i],
+                )
+
+        def quantise(name, staged, width):
+            codes = held(name + "_codes", [P, width], U32)
+            plane = held(name + "_plane", [P, width], U8)
+            nc.vector.quantize_mx(out=codes[:].bitcast(FP8X4), scales=plane[:], in_=staged)
+            return codes, plane
+
+        def round_weight(raw, sign, on_scalar):
+            staged = work.tile([P, 4 * PASS], BF16, name="staged", align_bytes=64)
+            dst = staged[:].rearrange("p (t g i j) -> p g t i j", t=4, i=4, j=4)
+            src = raw[:].rearrange("p j (g t i) -> p g t i j", t=4, i=4)
+            if on_scalar and sign > 0:
+                nc.scalar.copy(out=dst, in_=src)
+            elif on_scalar:
+                nc.scalar.activation(out=dst, in_=src, func=ACT.Copy, scale=sign)
+            else:
+                nc.vector.tensor_scalar(out=dst, in0=src, scalar1=sign, scalar2=None, op0=ALU.mult)
+            return staged[:]
+
+        def operand(pair, col, width):
+            codes, plane = pair
+            return codes[:, col : col + width].bitcast(FP8X4), plane[:, col : col + width]
+
+        def table_operand(a, c):
+            col = CHUNK * c
+            words = v0[:, col : col + CHUNK] if a == 0 else v1[col // HALF][:, col % HALF : col % HALF + CHUNK]
+            return words.bitcast(FP8X4), v_plane[a][:, col : col + CHUNK]
+
+        def w2_operand(a, b, t):
+            col = PASS * b + P * t
+            return w2_codes[:, a, 2 * col : 2 * (col + P)].bitcast(FP4X4), w2_plane[:, a, col : col + P]
+
+        def products(terms, u):
+            bank = psum.tile([P, 2, CHUNK], F32, name="bank")
+            for e in range(2):
+                pairs = terms(2 * u + e)
+                for n, (lhs, rhs) in enumerate(pairs):
+                    nc.tensor.matmul_mx(
+                        out=bank[:, e, :], lhsT=lhs[0], lhsT_scale=lhs[1], rhs=rhs[0], rhs_scale=rhs[1],
+                        start=(n == 0), stop=(n == len(pairs) - 1),
+                    )
+            return bank[:].rearrange("p e n -> p n e")
+
+        def paired(tile, u):
+            return tile[:, u, :].rearrange("p (n e) -> p n e", e=2)
+
+        xs_pair = (xs_codes, xs_plane)
+
+        w3_q = [quantise("w3_0", round_weight(w3_raw[0], 1.0, True), PASS)]
+        x_kept = []
+        for c in range(CHUNKS):
+            x_c = held("x_kept%d" % c, [P, 2, 2 * CHUNK], F32)
+            for u in range(2):
+                bank = products(lambda t: [(operand(w3_q[0], P * t, P), operand(xs_pair, CHUNK * c, CHUNK))], u)
+                nc.scalar.copy(out=paired(x_c, u), in_=bank)
+            x_kept.append(x_c)
+
+        nc.vector.tensor_copy(out=v0[:], in_=tab[0][:].indirect(offsets[:]))
+        nc.vector.tensor_copy(
+            out=w2_codes[:].rearrange("p a c -> p (a c)").bitcast(I32).rearrange("p (s t g w) -> p s t g w", t=4, g=32, w=2),
+            in_=w2_raw[:].rearrange("p a c -> p (a c)").bitcast(I32).rearrange("p (s g t w) -> p s t g w", t=4, g=32, w=2),
+        )
+        nc.vector.tensor_copy(
+            out=w2_plane[:].rearrange("p a c -> p (a c)").bitcast(I32).rearrange("p (s t g) -> p s t g", t=4, g=32),
+            in_=w2_raw_plane[:].rearrange("p a c -> p (a c)").bitcast(I32).rearrange("p (s g t) -> p s t g", t=4, g=32),
+        )
+        for n in range(2):
+            nc.vector.tensor_copy(out=v1[n][:], in_=tab[1][:].indirect(offsets[:, 32 * n : 32 * (n + 1)]))
+
+        def b_terms(b, c):
+            return lambda t: [(w2_operand(a, b, t), table_operand(a, c)) for a in range(2)]
+
+        def a_terms(w1_q, c):
+            return lambda t: [(operand(w1_q[a], P * t, P), table_operand(a, c)) for a in range(2)]
+
+        def with_x(terms, c):
+            return lambda t: terms(t) + [(operand(w3_q[1], P * t, P), operand(xs_pair, CHUNK * c, CHUNK))]
+
+        second = [[held("second%d%d" % (b, c), [P, 2, 2 * CHUNK], F32) for c in range(CHUNKS)] for b in range(2)]
+        h_codes = [held("h_codes%d" % b, [P, S], U32) for b in range(2)]
+        h_plane = [held("h_plane%d" % b, [P, S], U8) for b in range(2)]
+
+        w1_q = [quantise("w1_0%d" % a, round_weight(w1_raw[0][a], 1.0, True), PASS) for a in range(2)]
+        for c in range(CHUNKS):
+            for u in range(2):
+                bank = products(b_terms(0, c), u)
+                nc.vector.tensor_tensor(out=paired(second[0][c], u), in0=bank, in1=paired(x_kept[c], u), op=ALU.subtract)
+            nc.scalar.activation(out=second[0][c][:], in_=second[0][c][:], func=ACT.Tanh)
+
+        turned = psum.tile([P, P], F32, name="bank")
+        nc.tensor.transpose(turned[:], vec_rows[:], ident[:])
+        nc.scalar.copy(out=consts[:], in_=turned[:, 0:16])
+
+        first = {}
+        rounded = {}
+        w4_q = []
+
+        def first_tanh(b, c):
+            tile = work.tile([P, 2, 2 * CHUNK], F32, name="first", bufs=4)
+            for u in range(2):
+                if b == 0:
+                    bank = products(a_terms(w1_q, c), u)
+                    nc.vector.tensor_tensor(out=paired(tile, u), in0=bank, in1=paired(x_kept[c], u), op=ALU.add)
+                else:
+                    bank = products(with_x(a_terms(w1_q[2:], c), c), u)
+                    nc.scalar.activation(out=paired(tile, u), in_=bank, func=ACT.Tanh, scale=-1.0)
+            if b == 0:
+                nc.scalar.activation(out=tile[:], in_=tile[:], func=ACT.Tanh)
+            first[(b, c)] = tile
+
+        def second_tanh(c):
+            for u in range(2):
+                bank = products(with_x(b_terms(1, c), c), u)
+                nc.scalar.activation(out=paired(second[1][c], u), in_=bank, func=ACT.Tanh)
+
+        def difference(b, c):
+            tile = first[(b, c)]
+            nc.vector.tensor_tensor(out=tile[:], in0=tile[:], in1=second[b][c][:], op=ALU.subtract)
+
+        def apply_gain(b, c):
+            h = work.tile([P, 4 * CHUNK], BF16, name="h", align_bytes=64, bufs=2)
+            nc.vector.tensor_tensor(
+                out=h[:].rearrange("p (n u e) -> p n u e", u=2, e=2),
+                in0=first[(b, c)][:].rearrange("p u (n e) -> p n u e", e=2),
+                in1=consts[:, 4 * b : 4 * b + 4].rearrange("p (o u e) -> p o u e", o=1, e=2).to_broadcast([P, CHUNK, 2, 2]),
+                op=ALU.mult,
+            )
+            rounded[(b, c)] = h
+
+        def quantise_h(b, c):
+            cols = slice(CHUNK * c, CHUNK * (c + 1))
+            nc.vector.quantize_mx(
+                out=h_codes[b][:, cols].bitcast(FP8X4), scales=h_plane[b][:, cols], in_=rounded[(b, c)][:]
+            )
+
+        def scores(c):
+            bank = psum.tile([P, 2, CHUNK], F32, name="bank")
+            result = work.tile([P, 2, CHUNK], F32, name="result", bufs=2)
+            for m in range(2):
+                for b in range(2):
+                    lhs = operand(w4_q[0], N * b + P * m, P)
+                    rhs = operand((h_codes[b], h_plane[b]), CHUNK * c, CHUNK)
+                    nc.tensor.matmul_mx(
+                        out=bank[:, m, :], lhsT=lhs[0], lhsT_scale=lhs[1], rhs=rhs[0], rhs_scale=rhs[1],
+                        start=(b == 0), stop=(b == 1),
+                    )
+            for m in range(2):
+                nc.scalar.activation(
+                    out=result[:, m, :], in_=bank[:, m, :], func=ACT.Identity, bias=consts[:, 8 + m : 9 + m]
+                )
+            nc.sync.dma_start(
+                out=out[:, CHUNK * c : CHUNK * (c + 1)].rearrange("(m p) s -> p m s", p=P), in_=result[:]
+            )
+
+        def late_weight(n):
+            if n == 0:
+                w3_q.append(quantise("w3_1", round_weight(w3_raw[1], -1.0, True), PASS))
+            elif n < 3:
+                w1_q.append(quantise("w1_1%d" % n, round_weight(w1_raw[1][n - 1], -1.0, True), PASS))
+            else:
+                staged = work.tile([P, 4 * PASS], BF16, name="staged", align_bytes=64)
+                nc.scalar.copy(
+                    out=staged[:].rearrange("p (b n t) -> p b n t", b=2, t=4),
+                    in_=w4_raw[:].rearrange("p b t n -> p b n t"),
+                )
+                w4_q.append(quantise("w4", staged[:], 2 * N))
+
+        units = [(b, c) for b in range(2) for c in range(CHUNKS)]
+        for step in range(len(units) + 3):
+            if step < len(units):
+                first_tanh(*units[step])
+            if step < CHUNKS:
+                late_weight(step)
+                second_tanh(step)
+            if 0 <= step - 2 < len(units):
+                apply_gain(*units[step - 2])
+            if 0 <= step - 1 < len(units):
+                difference(*units[step - 1])
+            if 0 <= step - 2 < len(units):
+                quantise_h(*units[step - 2])
+                if units[step - 2][0] == 1:
+                    scores(units[step - 2][1])

@@ -22,6 +22,8 @@ PASS = 512
 CHUNK = 256
 CHUNKS = S // CHUNK
 HALF = 512
+TURNED = 2
+CASTS = [None, None, None, 1, 0]
 
 
 def tile_list_udder_health_scores_kernel(
@@ -30,99 +32,125 @@ def tile_list_udder_health_scores_kernel(
     nc = tc.nc
     with ExitStack() as ctx:
         keep = ctx.enter_context(tc.tile_pool(name="keep", bufs=1))
+        shared = ctx.enter_context(tc.tile_pool(name="shared", bufs=1))
         work = ctx.enter_context(tc.tile_pool(name="work", bufs=3))
         psum = ctx.enter_context(tc.psum_pool(name="psum", bufs=8))
 
+        def placed(name, shape, dtype, kib):
+            return shared.tile(shape, dtype, name=name, align_bytes=64, offset=1024 * kib)
+
         def held(name, shape, dtype):
-            return keep.tile(shape, dtype, name=name, align_bytes=64)
+            return keep.tile(shape, dtype, name=name, tag=name, align_bytes=64)
 
         offsets = keep.tile([P, S // 16], U16, name="offsets")
-        tab = [held("tab%d" % a, [P, T], U32) for a in range(2)]
-        tab_rows = held("tab_rows", [P, T], U8)
-        xs_codes = held("xs_codes", [P, S], U32)
+        tab = [placed("tab%d" % a, [P, T], U32, (32, 0)[a]) for a in range(2)]
+        tab_rows = placed("tab_rows", [P, T], U8, 14)
+        xs_codes = [held("xs_codes%d" % n, [P, HALF], U32) for n in range(2)]
         xs_plane = held("xs_plane", [P, S], U8)
-        w2_raw = held("w2_raw", [P, 2, 2 * H], U8)
-        w2_raw_plane = held("w2_raw_plane", [P, 2, H], U8)
-        w2_codes = held("w2_codes", [P, 2, 2 * H], U8)
+        w2_raw = [placed("w2_raw%d" % b, [P, 2, 2 * PASS], U8, (50, 48)[b]) for b in range(2)]
+        w2_raw_plane = placed("w2_raw_plane", [P, 2, H], U8, 48)
+        w2_codes = [held("w2_codes%d" % b, [P, 2, 2 * PASS], U8) for b in range(2)]
         w2_plane = held("w2_plane", [P, 2, H], U8)
         v_rows = held("v_rows", [P, S], U8)
         v_plane = [held("v_plane%d" % a, [P, S], U8) for a in range(2)]
         v0 = held("v0", [P, S], U32)
         v1 = [held("v1_%d" % n, [P, HALF], U32) for n in range(2)]
-        vec_rows = held("vec_rows", [P, P], F32)
+        gain_rows = held("gain_rows", [P, PASS], F32)
+        gain_dealt = held("gain_dealt", [P, PASS], F32)
+        bias = held("bias", [P, 2], F32)
         ident = held("ident", [P, P], F32)
-        consts = held("consts", [P, 16], F32)
-        w1_raw = [[held("w1_raw%d%d" % (b, a), [P, 4, PASS], F32) for a in range(2)] for b in range(2)]
-        w3_raw = [held("w3_raw%d" % b, [P, 4, PASS], F32) for b in range(2)]
-        w4_raw = held("w4_raw", [P, 2, 4, N], F32)
+        gains = held("gains", [P, 8], F32)
+        w1_raw = [[placed("w1_raw%d%d" % (b, a), [P, 4, PASS], F32, ((16, 24), (40, 0))[b][a]) for a in range(2)] for b in range(2)]
+        w3_raw = [placed("w3_raw%d" % b, [P, 4, PASS], F32, (24, 32)[b]) for b in range(2)]
+        w4_raw = placed("w4_raw", [P, 2, 4, N], F32, 8)
 
         nc.vector.memset(xs_plane[:].bitcast(I32), 0)
-        nc.gpsimd.memset(tab_rows[32:64, :].bitcast(I32), 0)
+        nc.vector.memset(tab_rows[32:64, :].bitcast(I32), 0)
         nc.vector.memset(tab_rows[64:128, :].bitcast(I32), 0)
         nc.vector.memset(w2_raw_plane[:].rearrange("p a c -> p (a c)").bitcast(I32), 0)
         for a in range(2):
             nc.vector.memset(v_plane[a][:].bitcast(I32), 0)
-        nc.vector.memset(vec_rows[:], 0.0)
+        nc.vector.memset(gain_rows[:], 0.0)
         make_identity(nc, ident[:])
 
         def load_weight(dst, src, a, b):
             rows = src[PASS * a : PASS * (a + 1), PASS * b : PASS * (b + 1)]
             nc.sync.dma_start(out=dst[:], in_=rows.rearrange("(p j) c -> p j c", j=4))
 
-        def load_words(dst, src, lo, hi):
-            words = src.rearrange("p t i -> p (t i)").bitcast(I32)
-            nc.sync.dma_start(out=dst[:].bitcast(I32)[:, lo:hi], in_=words[:, lo:hi])
+        def load_words(dst, src):
+            nc.sync.dma_start(out=dst.bitcast(I32), in_=src.rearrange("p t i -> p (t i)").bitcast(I32))
 
-        def move_rows(a, q):
-            row = 16 * a + 4 * q
+        def load_table(a, n):
+            cols = slice(T // 2 * n, T // 2 * (n + 1))
+            load_words(tab[a][:, cols], tab_words[a, :, cols, :])
+
+        def load_xs(n):
+            load_words(xs_codes[n][:], xs_words[0, :, HALF * n : HALF * (n + 1), :])
+
+        def move_rows(a, r):
             nc.sync.dma_start(
-                out=v_plane[a][32 * q : 32 * q + 4, :].bitcast(I32), in_=v_rows[row : row + 4, :].bitcast(I32)
+                out=v_plane[a][r:P:32, :].bitcast(I32), in_=v_rows[16 * a + r : 16 * a + 16 : 4, :].bitcast(I32)
+            )
+
+        def load_xs_plane(r):
+            nc.sync.dma_start(out=xs_plane[4 + r : P : 32, :].bitcast(I32), in_=xs_scales[0, r:16:4, :].bitcast(I32))
+
+        def load_w2_plane(r):
+            nc.sync.dma_start(
+                out=w2_raw_plane[r:P:32, :, :].bitcast(I32),
+                in_=w2_scales[:, r:16:4, :].rearrange("a q c -> q a c").bitcast(I32),
+            )
+
+        def load_w2(b):
+            nc.sync.dma_start(
+                out=w2_raw[b][:].bitcast(I32),
+                in_=w2_words[:, :, 2 * PASS * b : 2 * PASS * (b + 1)].rearrange("a p c -> p a c").bitcast(I32),
             )
 
         nc.sync.dma_start(
             out=tab_rows[0:32, :].bitcast(I32), in_=tab_scales.rearrange("a q t -> (a q) t").bitcast(I32)
         )
         nc.sync.dma_start(offsets[:], offs)
-        load_weight(w3_raw[0], w3, 0, 0)
-        for q in range(4):
-            nc.sync.dma_start(
-                out=xs_plane[32 * q : 32 * q + 4, :].bitcast(I32), in_=xs_scales[0, 4 * q : 4 * q + 4, :].bitcast(I32)
-            )
-        load_words(xs_codes, xs_words[0], 0, S)
-        load_words(tab[0], tab_words[0], 0, T // 2)
-        for q in range(4):
-            nc.sync.dma_start(
-                out=w2_raw_plane[32 * q : 32 * q + 4, :, :].bitcast(I32),
-                in_=w2_scales[:, 4 * q : 4 * q + 4, :].rearrange("a r c -> r a c").bitcast(I32),
-            )
-        load_words(tab[0], tab_words[0], T // 2, T)
         nc.vector.tensor_copy(out=v_rows[:], in_=tab_rows[:].indirect(offsets[:]))
-        for q in range(3):
-            move_rows(0, q)
-        nc.sync.dma_start(out=w2_raw[:].bitcast(I32), in_=w2_words.rearrange("a p c -> p a c").bitcast(I32))
+        load_weight(w3_raw[0], w3, 0, 0)
+        load_xs(0)
+        load_xs_plane(0)
+        load_xs_plane(1)
+        load_xs_plane(2)
+        load_xs_plane(3)
+        load_table(0, 0)
+        load_xs(1)
+        load_w2_plane(0)
+        load_w2_plane(1)
+        load_w2_plane(2)
+        load_w2_plane(3)
+        load_table(0, 1)
+        load_w2(0)
+        nc.sync.dma_start(out=gain_rows[0:2, :], in_=gain.rearrange("(b r) -> b r", b=2))
+        move_rows(0, 0)
+        move_rows(0, 1)
+        move_rows(0, 2)
+        load_table(1, 0)
         move_rows(0, 3)
         move_rows(1, 0)
-        load_words(tab[1], tab_words[1], 0, T // 2)
-        for q in range(1, 4):
-            move_rows(1, q)
-        load_words(tab[1], tab_words[1], T // 2, T)
-        for a in range(2):
-            load_weight(w1_raw[0][a], w1, a, 0)
-        for b in range(2):
-            nc.sync.dma_start(
-                out=vec_rows[4 * b : 4 * b + 4, :].rearrange("t (g i) -> t g i", i=4),
-                in_=gain[PASS * b : PASS * (b + 1)].rearrange("(g t i) -> t g i", t=4, i=4),
-            )
-        nc.sync.dma_start(out=vec_rows[8:10, :], in_=b4.rearrange("(m p) -> m p", p=P))
+        move_rows(1, 1)
+        move_rows(1, 2)
+        move_rows(1, 3)
+        load_table(1, 1)
+        load_weight(w1_raw[0][0], w1, 0, 0)
+        load_weight(w1_raw[0][1], w1, 1, 0)
+        load_w2(1)
         load_weight(w3_raw[1], w3, 0, 1)
-        for a in range(2):
-            load_weight(w1_raw[1][a], w1, a, 1)
+        load_weight(w1_raw[1][0], w1, 0, 1)
+        load_weight(w1_raw[1][1], w1, 1, 1)
         for b in range(2):
             for i in range(4):
                 nc.sync.dma_start(
                     out=w4_raw[i:P:4, b, :, :],
                     in_=w4[PASS * b : PASS * (b + 1), :].rearrange("(g t i) n -> i g t n", t=4, i=4)[i],
                 )
+        with nc.allow_non_contiguous_dma(reason="two bias values a partition"):
+            nc.sync.dma_start(out=bias[:], in_=b4.rearrange("(m p) -> p m", p=P))
 
         def quantise(name, staged, width):
             codes = held(name + "_codes", [P, width], U32)
@@ -130,30 +158,53 @@ def tile_list_udder_health_scores_kernel(
             nc.vector.quantize_mx(out=codes[:].bitcast(FP8X4), scales=plane[:], in_=staged)
             return codes, plane
 
-        def round_weight(raw, sign, on_scalar):
+        def round_weight(raw, sign, engine_copy=None):
             staged = work.tile([P, 4 * PASS], BF16, name="staged", align_bytes=64)
-            dst = staged[:].rearrange("p (t g i j) -> p g t i j", t=4, i=4, j=4)
-            src = raw[:].rearrange("p j (g t i) -> p g t i j", t=4, i=4)
-            if on_scalar and sign > 0:
-                nc.scalar.copy(out=dst, in_=src)
-            elif on_scalar:
-                nc.scalar.activation(out=dst, in_=src, func=ACT.Copy, scale=sign)
+            dst = staged[:].rearrange("p (t g i j) -> p g t j i", t=4, i=4, j=4)
+            src = raw[:].rearrange("p j (g t i) -> p g t j i", t=4, i=4)
+            if sign > 0:
+                engine_copy(out=dst, in_=src)
+            elif engine_copy is None:
+                for t in range(4):
+                    nc.scalar.activation(out=dst[:, :, t, :, :], in_=src[:, :, t, :, :], func=ACT.Copy, scale=sign)
             else:
-                nc.vector.tensor_scalar(out=dst, in0=src, scalar1=sign, scalar2=None, op0=ALU.mult)
+                for t in range(4):
+                    nc.vector.tensor_scalar(
+                        out=dst[:, :, t, :, :], in0=src[:, :, t, :, :], scalar1=sign, scalar2=None, op0=ALU.mult
+                    )
             return staged[:]
 
         def operand(pair, col, width):
             codes, plane = pair
             return codes[:, col : col + width].bitcast(FP8X4), plane[:, col : col + width]
 
-        def table_operand(a, c):
-            col = CHUNK * c
-            words = v0[:, col : col + CHUNK] if a == 0 else v1[col // HALF][:, col % HALF : col % HALF + CHUNK]
-            return words.bitcast(FP8X4), v_plane[a][:, col : col + CHUNK]
+        def table_operand(a, col, width):
+            words = v0[:, col : col + width] if a == 0 else v1[col // HALF][:, col % HALF : col % HALF + width]
+            return words.bitcast(FP8X4), v_plane[a][:, col : col + width]
 
-        def w2_operand(a, b, t):
-            col = PASS * b + P * t
-            return w2_codes[:, a, 2 * col : 2 * (col + P)].bitcast(FP4X4), w2_plane[:, a, col : col + P]
+        def w2_operand(a, col, width):
+            words = w2_codes[col // PASS][:, a, 2 * (col % PASS) : 2 * (col % PASS + width)]
+            return words.bitcast(FP4X4), w2_plane[:, a, col : col + width]
+
+        def narrow_products(terms, u):
+            bank = psum.tile([P, 4, P], F32, name="bank")
+            for t in range(4):
+                pairs = terms(t)
+                for n, (lhs, rhs) in enumerate(pairs):
+                    nc.tensor.matmul_mx(
+                        out=bank[:, t, :], lhsT=lhs[0], lhsT_scale=lhs[1],
+                        rhs=rhs[0][:, P * u : P * (u + 1)], rhs_scale=rhs[1][:, P * u : P * (u + 1)],
+                        start=(n == 0), stop=(n == len(pairs) - 1),
+                    )
+            return bank[:].rearrange("p t n -> p n t")
+
+        def late_tanh(tile, terms, c, scale):
+            for u in range(2):
+                if c == CHUNKS - 1:
+                    dst, bank = tile[:, u, :].rearrange("p (n t) -> p n t", t=4), narrow_products(terms, u)
+                else:
+                    dst, bank = paired(tile, u), products(terms, u)
+                nc.scalar.activation(out=dst, in_=bank, func=ACT.Tanh, scale=scale)
 
         def products(terms, u):
             bank = psum.tile([P, 2, CHUNK], F32, name="bank")
@@ -169,53 +220,88 @@ def tile_list_udder_health_scores_kernel(
         def paired(tile, u):
             return tile[:, u, :].rearrange("p (n e) -> p n e", e=2)
 
-        xs_pair = (xs_codes, xs_plane)
+        def xs_operand(col, width):
+            return xs_codes[col // HALF][:, col % HALF : col % HALF + width].bitcast(FP8X4), xs_plane[4:P, col : col + width]
 
-        w3_q = [quantise("w3_0", round_weight(w3_raw[0], 1.0, True), PASS)]
+        def turned_product(pairs):
+            bank = psum.tile([P, PASS], F32, name="bank")
+            for n, (lhs, rhs) in enumerate(pairs):
+                nc.tensor.matmul_mx(
+                    out=bank[:], lhsT=lhs[0], lhsT_scale=lhs[1], rhs=rhs[0], rhs_scale=rhs[1],
+                    start=(n == 0), stop=(n == len(pairs) - 1),
+                )
+            return bank[:]
+
+
+        w3_q = [quantise("w3_0", round_weight(w3_raw[0], 1.0, nc.scalar.copy), PASS)]
         x_kept = []
         for c in range(CHUNKS):
             x_c = held("x_kept%d" % c, [P, 2, 2 * CHUNK], F32)
             for u in range(2):
-                bank = products(lambda t: [(operand(w3_q[0], P * t, P), operand(xs_pair, CHUNK * c, CHUNK))], u)
-                nc.scalar.copy(out=paired(x_c, u), in_=bank)
+                if c < TURNED:
+                    bank = turned_product([(xs_operand(CHUNK * c + P * u, P), operand(w3_q[0], 0, PASS))])
+                    nc.scalar.copy(out=x_c[:, u, :], in_=bank)
+                else:
+                    bank = products(lambda t: [(operand(w3_q[0], P * t, P), xs_operand(CHUNK * c, CHUNK))], u)
+                    nc.scalar.copy(out=paired(x_c, u), in_=bank)
             x_kept.append(x_c)
 
-        nc.vector.tensor_copy(out=v0[:], in_=tab[0][:].indirect(offsets[:]))
         nc.vector.tensor_copy(
-            out=w2_codes[:].rearrange("p a c -> p (a c)").bitcast(I32).rearrange("p (s t g w) -> p s t g w", t=4, g=32, w=2),
-            in_=w2_raw[:].rearrange("p a c -> p (a c)").bitcast(I32).rearrange("p (s g t w) -> p s t g w", t=4, g=32, w=2),
+            out=gain_dealt[:].rearrange("p (t g i) -> p t g i", t=4, i=4),
+            in_=gain_rows[:].rearrange("p (g t i) -> p t g i", t=4, i=4),
         )
+        turned = psum.tile([P, 4, P], F32, name="bank")
+        for t in range(4):
+            nc.tensor.transpose(turned[:, t, :], gain_dealt[:, P * t : P * (t + 1)], ident[:])
+        nc.scalar.copy(
+            out=gains[:].rearrange("p (b t) -> p b t", t=4), in_=turned[:, :, 0:2].rearrange("p t b -> p b t")
+        )
+
+        nc.vector.tensor_copy(out=v0[:], in_=tab[0][:].indirect(offsets[:]))
+        def deal_w2(b):
+            nc.vector.tensor_copy(
+                out=w2_codes[b][:].bitcast(I32).rearrange("p a (t g w) -> p a t g w", t=4, w=2),
+                in_=w2_raw[b][:].bitcast(I32).rearrange("p a (g t w) -> p a t g w", t=4, w=2),
+            )
+
         nc.vector.tensor_copy(
             out=w2_plane[:].rearrange("p a c -> p (a c)").bitcast(I32).rearrange("p (s t g) -> p s t g", t=4, g=32),
             in_=w2_raw_plane[:].rearrange("p a c -> p (a c)").bitcast(I32).rearrange("p (s g t) -> p s t g", t=4, g=32),
         )
+        deal_w2(0)
         for n in range(2):
             nc.vector.tensor_copy(out=v1[n][:], in_=tab[1][:].indirect(offsets[:, 32 * n : 32 * (n + 1)]))
 
         def b_terms(b, c):
-            return lambda t: [(w2_operand(a, b, t), table_operand(a, c)) for a in range(2)]
+            return lambda t: [(w2_operand(a, PASS * b + P * t, P), table_operand(a, CHUNK * c, CHUNK)) for a in range(2)]
 
         def a_terms(w1_q, c):
-            return lambda t: [(operand(w1_q[a], P * t, P), table_operand(a, c)) for a in range(2)]
+            return lambda t: [(operand(w1_q[a], P * t, P), table_operand(a, CHUNK * c, CHUNK)) for a in range(2)]
 
         def with_x(terms, c):
-            return lambda t: terms(t) + [(operand(w3_q[1], P * t, P), operand(xs_pair, CHUNK * c, CHUNK))]
+            return lambda t: terms(t) + [(operand(w3_q[1], P * t, P), xs_operand(CHUNK * c, CHUNK))]
 
         second = [[held("second%d%d" % (b, c), [P, 2, 2 * CHUNK], F32) for c in range(CHUNKS)] for b in range(2)]
         h_codes = [held("h_codes%d" % b, [P, S], U32) for b in range(2)]
         h_plane = [held("h_plane%d" % b, [P, S], U8) for b in range(2)]
 
-        w1_q = [quantise("w1_0%d" % a, round_weight(w1_raw[0][a], 1.0, True), PASS) for a in range(2)]
+        w1_q = [quantise("w1_0%d" % a, round_weight(w1_raw[0][a], 1.0, (nc.scalar.copy, nc.vector.tensor_copy)[a]), PASS) for a in range(2)]
         for c in range(CHUNKS):
             for u in range(2):
-                bank = products(b_terms(0, c), u)
-                nc.vector.tensor_tensor(out=paired(second[0][c], u), in0=bank, in1=paired(x_kept[c], u), op=ALU.subtract)
+                if c < TURNED:
+                    bank = turned_product(
+                        [(table_operand(a, CHUNK * c + P * u, P), w2_operand(a, 0, PASS)) for a in range(2)]
+                    )
+                    nc.vector.tensor_tensor(out=second[0][c][:, u, :], in0=x_kept[c][:, u, :], in1=bank, op=ALU.subtract)
+                else:
+                    bank = products(b_terms(0, c), u)
+                    nc.vector.tensor_tensor(
+                        out=paired(second[0][c], u), in0=bank, in1=paired(x_kept[c], u), op=ALU.subtract
+                    )
             nc.scalar.activation(out=second[0][c][:], in_=second[0][c][:], func=ACT.Tanh)
 
-        turned = psum.tile([P, P], F32, name="bank")
-        nc.tensor.transpose(turned[:], vec_rows[:], ident[:])
-        nc.scalar.copy(out=consts[:], in_=turned[:, 0:16])
 
+        results = placed("results", [P, 2, S], F32, 16)
         first = {}
         rounded = {}
         w4_q = []
@@ -223,85 +309,124 @@ def tile_list_udder_health_scores_kernel(
         def first_tanh(b, c):
             tile = work.tile([P, 2, 2 * CHUNK], F32, name="first", bufs=4)
             for u in range(2):
-                if b == 0:
+                if b == 0 and c < TURNED:
+                    bank = turned_product(
+                        [(table_operand(a, CHUNK * c + P * u, P), operand(w1_q[a], 0, PASS)) for a in range(2)]
+                    )
+                    nc.vector.tensor_tensor(out=tile[:, u, :], in0=bank, in1=x_kept[c][:, u, :], op=ALU.add)
+                elif b == 0:
                     bank = products(a_terms(w1_q, c), u)
                     nc.vector.tensor_tensor(out=paired(tile, u), in0=bank, in1=paired(x_kept[c], u), op=ALU.add)
-                else:
-                    bank = products(with_x(a_terms(w1_q[2:], c), c), u)
-                    nc.scalar.activation(out=paired(tile, u), in_=bank, func=ACT.Tanh, scale=-1.0)
             if b == 0:
                 nc.scalar.activation(out=tile[:], in_=tile[:], func=ACT.Tanh)
+            else:
+                late_tanh(tile, with_x(a_terms(w1_q[2:], c), c), c, -1.0)
             first[(b, c)] = tile
 
         def second_tanh(c):
-            for u in range(2):
-                bank = products(with_x(b_terms(1, c), c), u)
-                nc.scalar.activation(out=paired(second[1][c], u), in_=bank, func=ACT.Tanh)
+            late_tanh(second[1][c], with_x(b_terms(1, c), c), c, 1.0)
 
-        def difference(b, c):
-            tile = first[(b, c)]
-            nc.vector.tensor_tensor(out=tile[:], in0=tile[:], in1=second[b][c][:], op=ALU.subtract)
+        def difference(b, lo, width):
+            c, cols = lo // CHUNK, slice(2 * (lo % CHUNK), 2 * (lo % CHUNK + width))
+            if b == 0 and c < TURNED:
+                banks = []
+                for u in range(2):
+                    bank = psum.tile([P, 4, P], F32, name="bank")
+                    for t in range(4):
+                        for n, tile in enumerate((second[0][c], first[(0, c)])):
+                            nc.tensor.matmul(
+                                bank[:, t, :], lhsT=tile[:, u, P * t : P * (t + 1)], rhs=ident[:],
+                                start=(n == 0), stop=(n == 1), is_transpose=True,
+                            )
+                    banks.append(bank)
+                first[(0, c)] = banks
+                return
+            if width == P:
+                part, other = first[(b, c)][:, lo % CHUNK // P, :], second[b][c][:, lo % CHUNK // P, :]
+            else:
+                part, other = first[(b, c)][:], second[b][c][:]
+            nc.vector.tensor_tensor(out=part, in0=part, in1=other, op=ALU.subtract)
 
-        def apply_gain(b, c):
-            h = work.tile([P, 4 * CHUNK], BF16, name="h", align_bytes=64, bufs=2)
+        def apply_gain(b, lo, width):
+            c, cols = lo // CHUNK, slice(2 * (lo % CHUNK), 2 * (lo % CHUNK + width))
+            h = work.tile([P, 4 * width], BF16, name="h", align_bytes=64, bufs=2)
+            rounded[(b, lo)] = h
+            if b == 0 and c < TURNED:
+                for u in range(2):
+                    nc.vector.tensor_tensor(
+                        out=h[:, PASS * u : PASS * (u + 1)].rearrange("p (n t) -> p n t", t=4),
+                        in0=first[(0, c)][u][:].rearrange("p t n -> p n t"),
+                        in1=gains[:, 0:4].rearrange("p (o t) -> p o t", o=1).to_broadcast([P, P, 4]),
+                        op=ALU.mult,
+                    )
+                return
+            if width == P:
+                diff = first[(b, c)][:, lo % CHUNK // P, :].rearrange("p (n u e) -> p n u e", u=2, e=2)
+            else:
+                diff = first[(b, c)][:].rearrange("p u (n e) -> p n u e", e=2)
             nc.vector.tensor_tensor(
                 out=h[:].rearrange("p (n u e) -> p n u e", u=2, e=2),
-                in0=first[(b, c)][:].rearrange("p u (n e) -> p n u e", e=2),
-                in1=consts[:, 4 * b : 4 * b + 4].rearrange("p (o u e) -> p o u e", o=1, e=2).to_broadcast([P, CHUNK, 2, 2]),
+                in0=diff,
+                in1=gains[:, 4 * b : 4 * b + 4].rearrange("p (o u e) -> p o u e", o=1, e=2).to_broadcast([P, width, 2, 2]),
                 op=ALU.mult,
             )
-            rounded[(b, c)] = h
 
-        def quantise_h(b, c):
-            cols = slice(CHUNK * c, CHUNK * (c + 1))
+        def quantise_h(b, lo, width):
+            cols = slice(lo, lo + width)
             nc.vector.quantize_mx(
-                out=h_codes[b][:, cols].bitcast(FP8X4), scales=h_plane[b][:, cols], in_=rounded[(b, c)][:]
+                out=h_codes[b][:, cols].bitcast(FP8X4), scales=h_plane[b][:, cols], in_=rounded[(b, lo)][:]
             )
 
-        def scores(c):
-            bank = psum.tile([P, 2, CHUNK], F32, name="bank")
-            result = work.tile([P, 2, CHUNK], F32, name="result", bufs=2)
+        def scores(lo, width):
+            result = results[:, :, lo : lo + width]
             for m in range(2):
+                bank = psum.tile([P, width], F32, name="bank")
                 for b in range(2):
                     lhs = operand(w4_q[0], N * b + P * m, P)
-                    rhs = operand((h_codes[b], h_plane[b]), CHUNK * c, CHUNK)
+                    rhs = operand((h_codes[b], h_plane[b]), lo, width)
                     nc.tensor.matmul_mx(
-                        out=bank[:, m, :], lhsT=lhs[0], lhsT_scale=lhs[1], rhs=rhs[0], rhs_scale=rhs[1],
+                        out=bank[:], lhsT=lhs[0], lhsT_scale=lhs[1], rhs=rhs[0], rhs_scale=rhs[1],
                         start=(b == 0), stop=(b == 1),
                     )
-            for m in range(2):
-                nc.scalar.activation(
-                    out=result[:, m, :], in_=bank[:, m, :], func=ACT.Identity, bias=consts[:, 8 + m : 9 + m]
-                )
-            nc.sync.dma_start(
-                out=out[:, CHUNK * c : CHUNK * (c + 1)].rearrange("(m p) s -> p m s", p=P), in_=result[:]
-            )
+                if m == 1 and lo + width == S:
+                    nc.vector.tensor_scalar(
+                        out=result[:, m, :], in0=bank[:], scalar1=bias[:, m : m + 1], scalar2=None, op0=ALU.add
+                    )
+                else:
+                    nc.scalar.activation(out=result[:, m, :], in_=bank[:], func=ACT.Identity, bias=bias[:, m : m + 1])
+            nc.sync.dma_start(out=out[:, lo : lo + width].rearrange("(m p) s -> p m s", p=P), in_=result)
 
         def late_weight(n):
             if n == 0:
-                w3_q.append(quantise("w3_1", round_weight(w3_raw[1], -1.0, True), PASS))
+                deal_w2(1)
+                w3_q.append(quantise("w3_1", round_weight(w3_raw[1], -1.0, CASTS[0]), PASS))
             elif n < 3:
-                w1_q.append(quantise("w1_1%d" % n, round_weight(w1_raw[1][n - 1], -1.0, True), PASS))
+                w1_q.append(quantise("w1_1%d" % n, round_weight(w1_raw[1][n - 1], -1.0, CASTS[n]), PASS))
             else:
                 staged = work.tile([P, 4 * PASS], BF16, name="staged", align_bytes=64)
-                nc.scalar.copy(
-                    out=staged[:].rearrange("p (b n t) -> p b n t", b=2, t=4),
-                    in_=w4_raw[:].rearrange("p b t n -> p b n t"),
-                )
+                for b in range(2):
+                    (nc.scalar.copy, nc.vector.tensor_copy)[CASTS[3 + b]](
+                        out=staged[:, 4 * N * b : 4 * N * (b + 1)].rearrange("p (n i t) -> p n t i", i=4, t=4),
+                        in_=w4_raw[:, b, :, :].rearrange("p t (n i) -> p n t i", i=4),
+                    )
                 w4_q.append(quantise("w4", staged[:], 2 * N))
 
-        units = [(b, c) for b in range(2) for c in range(CHUNKS)]
-        for step in range(len(units) + 3):
-            if step < len(units):
-                first_tanh(*units[step])
-            if step < CHUNKS:
+        pieces = [(b, CHUNK * c, CHUNK) for b in range(2) for c in range(CHUNKS)][:-1]
+        pieces.extend([(1, S - CHUNK, P), (1, S - P, P)])
+        for step in range(len(pieces) + 2):
+            if CHUNKS <= step < 2 * CHUNKS:
+                second_tanh(step - CHUNKS)
+            if step < 2 * CHUNKS:
+                first_tanh(step // CHUNKS, step % CHUNKS)
+            if step < 3:
                 late_weight(step)
-                second_tanh(step)
-            if 0 <= step - 2 < len(units):
-                apply_gain(*units[step - 2])
-            if 0 <= step - 1 < len(units):
-                difference(*units[step - 1])
-            if 0 <= step - 2 < len(units):
-                quantise_h(*units[step - 2])
-                if units[step - 2][0] == 1:
-                    scores(units[step - 2][1])
+            if step == CHUNKS + 1:
+                late_weight(3)
+            if 0 <= step - 2:
+                apply_gain(*pieces[step - 2])
+            if 0 <= step - 1 < len(pieces):
+                difference(*pieces[step - 1])
+            if 0 <= step - 2:
+                quantise_h(*pieces[step - 2])
+                if pieces[step - 2][0] == 1:
+                    scores(*pieces[step - 2][1:])

from contextlib import ExitStack

import concourse.mybir as mybir
from concourse.masks import make_identity

K, T, S, K2, H, N = 1024, 4096, 1024, 512, 1024, 256
FLOPS = 2 * S * H * (K + K + K2 + N)

F32 = mybir.dt.float32
BF16 = mybir.dt.bfloat16
I32 = mybir.dt.int32
U32 = mybir.dt.uint32
U16 = mybir.dt.uint16
U8 = mybir.dt.uint8
FP8X4 = mybir.dt.float8_e4m3fn_x4
FP4X4 = mybir.dt.float4_e2m1fn_x4
ACT = mybir.ActivationFunctionType
ALU = mybir.AluOpType

P = 128
PASS = 512
CHUNK = 256
CHUNKS = S // CHUNK
HALF = 512
TURNED = 2
CASTS = [None, None, None, 1, 0]


def tile_list_udder_health_scores_kernel(
    tc, tab_words, tab_scales, offs, xs_words, xs_scales, w1, w2_words, w2_scales, w3, gain, w4, b4, out
):
    nc = tc.nc
    with ExitStack() as ctx:
        keep = ctx.enter_context(tc.tile_pool(name="keep", bufs=1))
        shared = ctx.enter_context(tc.tile_pool(name="shared", bufs=1))
        work = ctx.enter_context(tc.tile_pool(name="work", bufs=3))
        psum = ctx.enter_context(tc.psum_pool(name="psum", bufs=8))

        def placed(name, shape, dtype, kib):
            return shared.tile(shape, dtype, name=name, align_bytes=64, offset=1024 * kib)

        def held(name, shape, dtype):
            return keep.tile(shape, dtype, name=name, tag=name, align_bytes=64)

        offsets = keep.tile([P, S // 16], U16, name="offsets")
        tab = [placed("tab%d" % a, [P, T], U32, (32, 0)[a]) for a in range(2)]
        tab_rows = placed("tab_rows", [P, T], U8, 14)
        xs_codes = [held("xs_codes%d" % n, [P, HALF], U32) for n in range(2)]
        xs_plane = held("xs_plane", [P, S], U8)
        w2_raw = [placed("w2_raw%d" % b, [P, 2, 2 * PASS], U8, (50, 48)[b]) for b in range(2)]
        w2_raw_plane = placed("w2_raw_plane", [P, 2, H], U8, 48)
        w2_codes = [held("w2_codes%d" % b, [P, 2, 2 * PASS], U8) for b in range(2)]
        w2_plane = held("w2_plane", [P, 2, H], U8)
        v_rows = held("v_rows", [P, S], U8)
        v_plane = [held("v_plane%d" % a, [P, S], U8) for a in range(2)]
        v0 = held("v0", [P, S], U32)
        v1 = [held("v1_%d" % n, [P, HALF], U32) for n in range(2)]
        gain_rows = held("gain_rows", [P, PASS], F32)
        gain_dealt = held("gain_dealt", [P, PASS], F32)
        bias = held("bias", [P, 2], F32)
        ident = held("ident", [P, P], F32)
        gains = held("gains", [P, 8], F32)
        w1_raw = [[placed("w1_raw%d%d" % (b, a), [P, 4, PASS], F32, ((16, 24), (40, 0))[b][a]) for a in range(2)] for b in range(2)]
        w3_raw = [placed("w3_raw%d" % b, [P, 4, PASS], F32, (24, 32)[b]) for b in range(2)]
        w4_raw = placed("w4_raw", [P, 2, 4, N], F32, 8)

        nc.vector.memset(xs_plane[:].bitcast(I32), 0)
        nc.vector.memset(tab_rows[32:64, :].bitcast(I32), 0)
        nc.vector.memset(tab_rows[64:128, :].bitcast(I32), 0)
        nc.vector.memset(w2_raw_plane[:].rearrange("p a c -> p (a c)").bitcast(I32), 0)
        for a in range(2):
            nc.vector.memset(v_plane[a][:].bitcast(I32), 0)
        nc.vector.memset(gain_rows[:], 0.0)
        make_identity(nc, ident[:])

        def load_weight(dst, src, a, b):
            rows = src[PASS * a : PASS * (a + 1), PASS * b : PASS * (b + 1)]
            nc.sync.dma_start(out=dst[:], in_=rows.rearrange("(p j) c -> p j c", j=4))

        def load_words(dst, src):
            nc.sync.dma_start(out=dst.bitcast(I32), in_=src.rearrange("p t i -> p (t i)").bitcast(I32))

        def load_table(a, n):
            cols = slice(T // 2 * n, T // 2 * (n + 1))
            load_words(tab[a][:, cols], tab_words[a, :, cols, :])

        def load_xs(n):
            load_words(xs_codes[n][:], xs_words[0, :, HALF * n : HALF * (n + 1), :])

        def move_rows(a, r):
            nc.sync.dma_start(
                out=v_plane[a][r:P:32, :].bitcast(I32), in_=v_rows[16 * a + r : 16 * a + 16 : 4, :].bitcast(I32)
            )

        def load_xs_plane(r):
            nc.sync.dma_start(out=xs_plane[4 + r : P : 32, :].bitcast(I32), in_=xs_scales[0, r:16:4, :].bitcast(I32))

        def load_w2_plane(r):
            nc.sync.dma_start(
                out=w2_raw_plane[r:P:32, :, :].bitcast(I32),
                in_=w2_scales[:, r:16:4, :].rearrange("a q c -> q a c").bitcast(I32),
            )

        def load_w2(b):
            nc.sync.dma_start(
                out=w2_raw[b][:].bitcast(I32),
                in_=w2_words[:, :, 2 * PASS * b : 2 * PASS * (b + 1)].rearrange("a p c -> p a c").bitcast(I32),
            )

        nc.sync.dma_start(
            out=tab_rows[0:32, :].bitcast(I32), in_=tab_scales.rearrange("a q t -> (a q) t").bitcast(I32)
        )
        nc.sync.dma_start(offsets[:], offs)
        nc.vector.tensor_copy(out=v_rows[:], in_=tab_rows[:].indirect(offsets[:]))
        load_weight(w3_raw[0], w3, 0, 0)
        load_xs(0)
        load_xs_plane(0)
        load_xs_plane(1)
        load_xs_plane(2)
        load_xs_plane(3)
        load_table(0, 0)
        load_xs(1)
        load_w2_plane(0)
        load_w2_plane(1)
        load_w2_plane(2)
        load_w2_plane(3)
        load_table(0, 1)
        load_w2(0)
        nc.sync.dma_start(out=gain_rows[0:2, :], in_=gain.rearrange("(b r) -> b r", b=2))
        move_rows(0, 0)
        move_rows(0, 1)
        move_rows(0, 2)
        load_table(1, 0)
        move_rows(0, 3)
        move_rows(1, 0)
        move_rows(1, 1)
        move_rows(1, 2)
        move_rows(1, 3)
        load_table(1, 1)
        load_weight(w1_raw[0][0], w1, 0, 0)
        load_weight(w1_raw[0][1], w1, 1, 0)
        load_w2(1)
        load_weight(w3_raw[1], w3, 0, 1)
        load_weight(w1_raw[1][0], w1, 0, 1)
        load_weight(w1_raw[1][1], w1, 1, 1)
        for b in range(2):
            for i in range(4):
                nc.sync.dma_start(
                    out=w4_raw[i:P:4, b, :, :],
                    in_=w4[PASS * b : PASS * (b + 1), :].rearrange("(g t i) n -> i g t n", t=4, i=4)[i],
                )
        with nc.allow_non_contiguous_dma(reason="two bias values a partition"):
            nc.sync.dma_start(out=bias[:], in_=b4.rearrange("(m p) -> p m", p=P))

        def quantise(name, staged, width):
            codes = held(name + "_codes", [P, width], U32)
            plane = held(name + "_plane", [P, width], U8)
            nc.vector.quantize_mx(out=codes[:].bitcast(FP8X4), scales=plane[:], in_=staged)
            return codes, plane

        def round_weight(raw, sign, engine_copy=None):
            staged = work.tile([P, 4 * PASS], BF16, name="staged", align_bytes=64)
            dst = staged[:].rearrange("p (t g i j) -> p g t j i", t=4, i=4, j=4)
            src = raw[:].rearrange("p j (g t i) -> p g t j i", t=4, i=4)
            if sign > 0:
                engine_copy(out=dst, in_=src)
            elif engine_copy is None:
                for t in range(4):
                    nc.scalar.activation(out=dst[:, :, t, :, :], in_=src[:, :, t, :, :], func=ACT.Copy, scale=sign)
            else:
                for t in range(4):
                    nc.vector.tensor_scalar(
                        out=dst[:, :, t, :, :], in0=src[:, :, t, :, :], scalar1=sign, scalar2=None, op0=ALU.mult
                    )
            return staged[:]

        def operand(pair, col, width):
            codes, plane = pair
            return codes[:, col : col + width].bitcast(FP8X4), plane[:, col : col + width]

        def table_operand(a, col, width):
            words = v0[:, col : col + width] if a == 0 else v1[col // HALF][:, col % HALF : col % HALF + width]
            return words.bitcast(FP8X4), v_plane[a][:, col : col + width]

        def w2_operand(a, col, width):
            words = w2_codes[col // PASS][:, a, 2 * (col % PASS) : 2 * (col % PASS + width)]
            return words.bitcast(FP4X4), w2_plane[:, a, col : col + width]

        def narrow_products(terms, u):
            bank = psum.tile([P, 4, P], F32, name="bank")
            for t in range(4):
                pairs = terms(t)
                for n, (lhs, rhs) in enumerate(pairs):
                    nc.tensor.matmul_mx(
                        out=bank[:, t, :], lhsT=lhs[0], lhsT_scale=lhs[1],
                        rhs=rhs[0][:, P * u : P * (u + 1)], rhs_scale=rhs[1][:, P * u : P * (u + 1)],
                        start=(n == 0), stop=(n == len(pairs) - 1),
                    )
            return bank[:].rearrange("p t n -> p n t")

        def late_tanh(tile, terms, c, scale):
            for u in range(2):
                if c == CHUNKS - 1:
                    dst, bank = tile[:, u, :].rearrange("p (n t) -> p n t", t=4), narrow_products(terms, u)
                else:
                    dst, bank = paired(tile, u), products(terms, u)
                nc.scalar.activation(out=dst, in_=bank, func=ACT.Tanh, scale=scale)

        def products(terms, u):
            bank = psum.tile([P, 2, CHUNK], F32, name="bank")
            for e in range(2):
                pairs = terms(2 * u + e)
                for n, (lhs, rhs) in enumerate(pairs):
                    nc.tensor.matmul_mx(
                        out=bank[:, e, :], lhsT=lhs[0], lhsT_scale=lhs[1], rhs=rhs[0], rhs_scale=rhs[1],
                        start=(n == 0), stop=(n == len(pairs) - 1),
                    )
            return bank[:].rearrange("p e n -> p n e")

        def paired(tile, u):
            return tile[:, u, :].rearrange("p (n e) -> p n e", e=2)

        def xs_operand(col, width):
            return xs_codes[col // HALF][:, col % HALF : col % HALF + width].bitcast(FP8X4), xs_plane[4:P, col : col + width]

        def turned_product(pairs):
            bank = psum.tile([P, PASS], F32, name="bank")
            for n, (lhs, rhs) in enumerate(pairs):
                nc.tensor.matmul_mx(
                    out=bank[:], lhsT=lhs[0], lhsT_scale=lhs[1], rhs=rhs[0], rhs_scale=rhs[1],
                    start=(n == 0), stop=(n == len(pairs) - 1),
                )
            return bank[:]


        w3_q = [quantise("w3_0", round_weight(w3_raw[0], 1.0, nc.scalar.copy), PASS)]
        x_kept = []
        for c in range(CHUNKS):
            x_c = held("x_kept%d" % c, [P, 2, 2 * CHUNK], F32)
            for u in range(2):
                if c < TURNED:
                    bank = turned_product([(xs_operand(CHUNK * c + P * u, P), operand(w3_q[0], 0, PASS))])
                    nc.scalar.copy(out=x_c[:, u, :], in_=bank)
                else:
                    bank = products(lambda t: [(operand(w3_q[0], P * t, P), xs_operand(CHUNK * c, CHUNK))], u)
                    nc.scalar.copy(out=paired(x_c, u), in_=bank)
            x_kept.append(x_c)

        nc.vector.tensor_copy(
            out=gain_dealt[:].rearrange("p (t g i) -> p t g i", t=4, i=4),
            in_=gain_rows[:].rearrange("p (g t i) -> p t g i", t=4, i=4),
        )
        turned = psum.tile([P, 4, P], F32, name="bank")
        for t in range(4):
            nc.tensor.transpose(turned[:, t, :], gain_dealt[:, P * t : P * (t + 1)], ident[:])
        nc.scalar.copy(
            out=gains[:].rearrange("p (b t) -> p b t", t=4), in_=turned[:, :, 0:2].rearrange("p t b -> p b t")
        )

        nc.vector.tensor_copy(out=v0[:], in_=tab[0][:].indirect(offsets[:]))
        def deal_w2(b):
            nc.vector.tensor_copy(
                out=w2_codes[b][:].bitcast(I32).rearrange("p a (t g w) -> p a t g w", t=4, w=2),
                in_=w2_raw[b][:].bitcast(I32).rearrange("p a (g t w) -> p a t g w", t=4, w=2),
            )

        nc.vector.tensor_copy(
            out=w2_plane[:].rearrange("p a c -> p (a c)").bitcast(I32).rearrange("p (s t g) -> p s t g", t=4, g=32),
            in_=w2_raw_plane[:].rearrange("p a c -> p (a c)").bitcast(I32).rearrange("p (s g t) -> p s t g", t=4, g=32),
        )
        deal_w2(0)
        for n in range(2):
            nc.vector.tensor_copy(out=v1[n][:], in_=tab[1][:].indirect(offsets[:, 32 * n : 32 * (n + 1)]))

        def b_terms(b, c):
            return lambda t: [(w2_operand(a, PASS * b + P * t, P), table_operand(a, CHUNK * c, CHUNK)) for a in range(2)]

        def a_terms(w1_q, c):
            return lambda t: [(operand(w1_q[a], P * t, P), table_operand(a, CHUNK * c, CHUNK)) for a in range(2)]

        def with_x(terms, c):
            return lambda t: terms(t) + [(operand(w3_q[1], P * t, P), xs_operand(CHUNK * c, CHUNK))]

        second = [[held("second%d%d" % (b, c), [P, 2, 2 * CHUNK], F32) for c in range(CHUNKS)] for b in range(2)]
        h_codes = [held("h_codes%d" % b, [P, S], U32) for b in range(2)]
        h_plane = [held("h_plane%d" % b, [P, S], U8) for b in range(2)]

        w1_q = [quantise("w1_0%d" % a, round_weight(w1_raw[0][a], 1.0, (nc.scalar.copy, nc.vector.tensor_copy)[a]), PASS) for a in range(2)]
        for c in range(CHUNKS):
            for u in range(2):
                if c < TURNED:
                    bank = turned_product(
                        [(table_operand(a, CHUNK * c + P * u, P), w2_operand(a, 0, PASS)) for a in range(2)]
                    )
                    nc.vector.tensor_tensor(out=second[0][c][:, u, :], in0=x_kept[c][:, u, :], in1=bank, op=ALU.subtract)
                else:
                    bank = products(b_terms(0, c), u)
                    nc.vector.tensor_tensor(
                        out=paired(second[0][c], u), in0=bank, in1=paired(x_kept[c], u), op=ALU.subtract
                    )
            nc.scalar.activation(out=second[0][c][:], in_=second[0][c][:], func=ACT.Tanh)


        results = placed("results", [P, 2, S], F32, 16)
        first = {}
        rounded = {}
        w4_q = []

        def first_tanh(b, c):
            tile = work.tile([P, 2, 2 * CHUNK], F32, name="first", bufs=4)
            for u in range(2):
                if b == 0 and c < TURNED:
                    bank = turned_product(
                        [(table_operand(a, CHUNK * c + P * u, P), operand(w1_q[a], 0, PASS)) for a in range(2)]
                    )
                    nc.vector.tensor_tensor(out=tile[:, u, :], in0=bank, in1=x_kept[c][:, u, :], op=ALU.add)
                elif b == 0:
                    bank = products(a_terms(w1_q, c), u)
                    nc.vector.tensor_tensor(out=paired(tile, u), in0=bank, in1=paired(x_kept[c], u), op=ALU.add)
            if b == 0:
                nc.scalar.activation(out=tile[:], in_=tile[:], func=ACT.Tanh)
            else:
                late_tanh(tile, with_x(a_terms(w1_q[2:], c), c), c, -1.0)
            first[(b, c)] = tile

        def second_tanh(c):
            late_tanh(second[1][c], with_x(b_terms(1, c), c), c, 1.0)

        def difference(b, lo, width):
            c, cols = lo // CHUNK, slice(2 * (lo % CHUNK), 2 * (lo % CHUNK + width))
            if b == 0 and c < TURNED:
                banks = []
                for u in range(2):
                    bank = psum.tile([P, 4, P], F32, name="bank")
                    for t in range(4):
                        for n, tile in enumerate((second[0][c], first[(0, c)])):
                            nc.tensor.matmul(
                                bank[:, t, :], lhsT=tile[:, u, P * t : P * (t + 1)], rhs=ident[:],
                                start=(n == 0), stop=(n == 1), is_transpose=True,
                            )
                    banks.append(bank)
                first[(0, c)] = banks
                return
            if width == P:
                part, other = first[(b, c)][:, lo % CHUNK // P, :], second[b][c][:, lo % CHUNK // P, :]
            else:
                part, other = first[(b, c)][:], second[b][c][:]
            nc.vector.tensor_tensor(out=part, in0=part, in1=other, op=ALU.subtract)

        def apply_gain(b, lo, width):
            c, cols = lo // CHUNK, slice(2 * (lo % CHUNK), 2 * (lo % CHUNK + width))
            h = work.tile([P, 4 * width], BF16, name="h", align_bytes=64, bufs=2)
            rounded[(b, lo)] = h
            if b == 0 and c < TURNED:
                for u in range(2):
                    nc.vector.tensor_tensor(
                        out=h[:, PASS * u : PASS * (u + 1)].rearrange("p (n t) -> p n t", t=4),
                        in0=first[(0, c)][u][:].rearrange("p t n -> p n t"),
                        in1=gains[:, 0:4].rearrange("p (o t) -> p o t", o=1).to_broadcast([P, P, 4]),
                        op=ALU.mult,
                    )
                return
            if width == P:
                diff = first[(b, c)][:, lo % CHUNK // P, :].rearrange("p (n u e) -> p n u e", u=2, e=2)
            else:
                diff = first[(b, c)][:].rearrange("p u (n e) -> p n u e", e=2)
            nc.vector.tensor_tensor(
                out=h[:].rearrange("p (n u e) -> p n u e", u=2, e=2),
                in0=diff,
                in1=gains[:, 4 * b : 4 * b + 4].rearrange("p (o u e) -> p o u e", o=1, e=2).to_broadcast([P, width, 2, 2]),
                op=ALU.mult,
            )

        def quantise_h(b, lo, width):
            cols = slice(lo, lo + width)
            nc.vector.quantize_mx(
                out=h_codes[b][:, cols].bitcast(FP8X4), scales=h_plane[b][:, cols], in_=rounded[(b, lo)][:]
            )

        def scores(lo, width):
            result = results[:, :, lo : lo + width]
            for m in range(2):
                bank = psum.tile([P, width], F32, name="bank")
                for b in range(2):
                    lhs = operand(w4_q[0], N * b + P * m, P)
                    rhs = operand((h_codes[b], h_plane[b]), lo, width)
                    nc.tensor.matmul_mx(
                        out=bank[:], lhsT=lhs[0], lhsT_scale=lhs[1], rhs=rhs[0], rhs_scale=rhs[1],
                        start=(b == 0), stop=(b == 1),
                    )
                if m == 1 and lo + width == S:
                    nc.vector.tensor_scalar(
                        out=result[:, m, :], in0=bank[:], scalar1=bias[:, m : m + 1], scalar2=None, op0=ALU.add
                    )
                else:
                    nc.scalar.activation(out=result[:, m, :], in_=bank[:], func=ACT.Identity, bias=bias[:, m : m + 1])
            nc.sync.dma_start(out=out[:, lo : lo + width].rearrange("(m p) s -> p m s", p=P), in_=result)

        def late_weight(n):
            if n == 0:
                deal_w2(1)
                w3_q.append(quantise("w3_1", round_weight(w3_raw[1], -1.0, CASTS[0]), PASS))
            elif n < 3:
                w1_q.append(quantise("w1_1%d" % n, round_weight(w1_raw[1][n - 1], -1.0, CASTS[n]), PASS))
            else:
                staged = work.tile([P, 4 * PASS], BF16, name="staged", align_bytes=64)
                for b in range(2):
                    (nc.scalar.copy, nc.vector.tensor_copy)[CASTS[3 + b]](
                        out=staged[:, 4 * N * b : 4 * N * (b + 1)].rearrange("p (n i t) -> p n t i", i=4, t=4),
                        in_=w4_raw[:, b, :, :].rearrange("p t (n i) -> p n t i", i=4),
                    )
                w4_q.append(quantise("w4", staged[:], 2 * N))

        pieces = [(b, CHUNK * c, CHUNK) for b in range(2) for c in range(CHUNKS)][:-1]
        pieces.extend([(1, S - CHUNK, P), (1, S - P, P)])
        for step in range(len(pieces) + 2):
            if CHUNKS <= step < 2 * CHUNKS:
                second_tanh(step - CHUNKS)
            if step < 2 * CHUNKS:
                first_tanh(step // CHUNKS, step % CHUNKS)
            if step < 3:
                late_weight(step)
            if step == CHUNKS + 1:
                late_weight(3)
            if 0 <= step - 2:
                apply_gain(*pieces[step - 2])
            if 0 <= step - 1 < len(pieces):
                difference(*pieces[step - 1])
            if 0 <= step - 2:
                quantise_h(*pieces[step - 2])
                if pieces[step - 2][0] == 1:
                    scores(*pieces[step - 2][1:])
